import numpy as np
CORES = [0,1,16,17,32,33,48,49,64,65,80,81,96,97,112,113,136,137,152,153,168,169,184,185,200,201,216,217,232,233,248,249]
N = 32
def setup_inputs(rng):
    return {"x": rng.standard_normal((N, 128, 1024)).astype(np.float32)}
def reference(x):
    b = 1024 // N
    blocks = x.reshape(N, 128, N, b)
    return {"y": np.ascontiguousarray(blocks.transpose(2, 1, 0, 3)).reshape(N, 128, 1024)}

@@ -1,0 +1,115 @@
+from concourse.bass import DstId, RemoteDMATransfer
+
+NB = 32
+B = 32
+
+SCRATCH = {
+    "src": ("sbuf", [128, NB * B], "float32"),
+    "land": ("sbuf", [128, NB * B], "float32"),
+}
+SEMAPHORES = ["loaded", "own", "sent", "arrived", "stored"]
+
+MATE_PORT = (2, 3, 6, 7)
+
+
+def world(host, chip, core):
+    return host * 128 + chip * 8 + core
+
+
+def rank_core(r):
+    h, k, c = r // 16, (r % 16) // 2, r % 2
+    return world(h, 2 * k + h, c)
+
+
+def plan():
+    writes = {}
+    used = {}
+
+    def put(core, dst, src_col, dst_col, n):
+        writes.setdefault(core, []).append((dst, src_col, dst_col, n))
+
+    def via(r, helper, first, n):
+        slot = used.get(helper, 0)
+        used[helper] = slot + n * B
+        put(rank_core(r), helper, first * B, slot, n)
+        for i in range(n):
+            put(helper, rank_core(first + i), slot + i * B, r * B, 1)
+
+    for r in range(NB):
+        h, k, c = r // 16, (r % 16) // 2, r % 2
+        chip = 2 * k + h
+        mine, other = 16 * h, 16 * (1 - h)
+        die_a, die_b, die_b_port = world(h, chip, 2 + c), world(h, chip, 4 + c), world(h, chip, 6 + c)
+        put(rank_core(r), rank_core(r ^ 1), (r ^ 1) * B, r * B, 1)
+        via(r, die_a if c == 0 else die_b_port, mine + 2 * (k ^ 1), 2)
+        pair = k // 2
+        via(r, die_a, mine + 4 * ((pair + 1) % 4), 4)
+        via(r, die_b, mine + 4 * ((pair + 2) % 4), 4)
+        via(r, die_b, mine + 4 * ((pair + 3) % 4), 4)
+        half = k // 4
+        base = other + 8 * half
+        via(r, die_a, base + 4 * c, 4)
+        via(r, die_b_port, base + 4 * (1 - c), 4)
+        for m in range(4 * (1 - half), 4 * (1 - half) + 4):
+            via(r, world(1 - h, 2 * m + h, MATE_PORT[k % 4]), other + 2 * m, 2)
+    return writes
+
+
+def calls_of(core, writes):
+    calls = []
+    for n in sorted({w[3] for w in writes}):
+        off = [w for w in writes if w[3] == n and w[0] // 8 != core // 8]
+        on = [w for w in writes if w[3] == n and w[0] // 8 == core // 8]
+        while off or on:
+            take_off, off = off[:8], off[8:]
+            e_off = 8
+            while take_off and e_off * len(take_off) > 8:
+                e_off //= 2
+            first_on = e_off * len(take_off)
+            take_on, on = on[:16 - first_on], on[16 - first_on:]
+            e_on = 16
+            while take_on and e_on * len(take_on) > 16 - first_on:
+                e_on //= 2
+            call, bit = [], 0
+            for group, e in ((take_off, e_off), (take_on, e_on)):
+                for w in group:
+                    call.append(w + (((1 << e) - 1) << bit, e))
+                    bit += e
+            calls.append(call)
+    return calls
+
+
+def rank_program(g, core, T, topo):
+    writes = plan()
+    all_calls = {c: calls_of(c, w) for c, w in writes.items()}
+    if core not in all_calls:
+        return
+    arriving = sum(t[5] for calls in all_calls.values() for call in calls for t in call if t[0] == core)
+    rank = T.rank_of(core)
+
+    if rank is not None:
+        g.dma_start(T.src[:], T.x[:]).then_inc(T.sem.loaded, 16)
+        g.dma_start(T.land[:, rank * B:(rank + 1) * B], T.x[:, rank * B:(rank + 1) * B]).then_inc(T.sem.own, 16)
+        g.wait_ge(T.sem.loaded, 16)
+        source = T.src
+    else:
+        g.wait_ge(T.sem.arrived, arriving)
+        source = T.land
+
+    leaving = 0
+    for call in all_calls[core]:
+        transfers = []
+        for dst, src_col, dst_col, n, mask, engines in call:
+            rid, pid = topo.addr(dst, core)
+            transfers.append(RemoteDMATransfer(
+                dst_ids=[DstId(rid=rid, pnc=pid)], dma_engine_mask=mask, remote_sem=T.sem.arrived,
+                src=source[:, src_col:src_col + n * B], dst=T.land[:, dst_col:dst_col + n * B]))
+            leaving += engines
+        g.remote_dma_fused(transfers, local_sem=T.sem.sent)
+
+    if rank is not None:
+        g.wait_ge(T.sem.arrived, arriving)
+        g.wait_ge(T.sem.own, 16)
+        g.dma_start(T.y[:], T.land[:]).then_inc(T.sem.stored, 16)
+        g.wait_ge(T.sem.stored, 16)
+    g.wait_ge(T.sem.sent, leaving)

@@ -39,18 +39,14 @@ def plan():
         h, k, c = r // 16, (r % 16) // 2, r % 2
         chip = 2 * k + h
         mine, other = 16 * h, 16 * (1 - h)
-        die_a, die_b, die_b_port = world(h, chip, 2 + c), world(h, chip, 4 + c), world(h, chip, 6 + c)
+        group = k // 4
         put(rank_core(r), rank_core(r ^ 1), (r ^ 1) * B, r * B, 1)
-        via(r, die_a if c == 0 else die_b_port, mine + 2 * (k ^ 1), 2)
-        pair = k // 2
-        via(r, die_a, mine + 4 * ((pair + 1) % 4), 4)
-        via(r, die_b, mine + 4 * ((pair + 2) % 4), 4)
-        via(r, die_b, mine + 4 * ((pair + 3) % 4), 4)
-        half = k // 4
-        base = other + 8 * half
-        via(r, die_a, base + 4 * c, 4)
-        via(r, die_b_port, base + 4 * (1 - c), 4)
-        for m in range(4 * (1 - half), 4 * (1 - half) + 4):
+        for k2 in range(4 * group, 4 * group + 4):
+            if k2 != k:
+                via(r, world(h, chip, 7 if (c == 1 and k2 == k ^ 1) else 3), mine + 2 * k2, 2)
+        via(r, world(h, chip, 4 + c), mine + 8 * (1 - group), 8)
+        via(r, world(h, chip, 2 if c == 0 else 6), other + 8 * group, 8)
+        for m in range(4 * (1 - group), 4 * (1 - group) + 4):
             via(r, world(1 - h, 2 * m + h, MATE_PORT[k % 4]), other + 2 * m, 2)
     return writes
 

from concourse.bass import DstId, RemoteDMATransfer

NB = 32
B = 32

SCRATCH = {
    "src": ("sbuf", [128, NB * B], "float32"),
    "land": ("sbuf", [128, NB * B], "float32"),
}
SEMAPHORES = ["loaded", "own", "sent", "arrived", "stored"]

MATE_PORT = (2, 3, 6, 7)


def world(host, chip, core):
    return host * 128 + chip * 8 + core


def rank_core(r):
    h, k, c = r // 16, (r % 16) // 2, r % 2
    return world(h, 2 * k + h, c)


def plan():
    writes = {}
    used = {}

    def put(core, dst, src_col, dst_col, n):
        writes.setdefault(core, []).append((dst, src_col, dst_col, n))

    def via(r, helper, first, n):
        slot = used.get(helper, 0)
        used[helper] = slot + n * B
        put(rank_core(r), helper, first * B, slot, n)
        for i in range(n):
            put(helper, rank_core(first + i), slot + i * B, r * B, 1)

    for r in range(NB):
        h, k, c = r // 16, (r % 16) // 2, r % 2
        chip = 2 * k + h
        mine, other = 16 * h, 16 * (1 - h)
        group = k // 4
        put(rank_core(r), rank_core(r ^ 1), (r ^ 1) * B, r * B, 1)
        for k2 in range(4 * group, 4 * group + 4):
            if k2 != k:
                via(r, world(h, chip, 7 if (c == 1 and k2 == k ^ 1) else 3), mine + 2 * k2, 2)
        via(r, world(h, chip, 4 + c), mine + 8 * (1 - group), 8)
        via(r, world(h, chip, 2 if c == 0 else 6), other + 8 * group, 8)
        for m in range(4 * (1 - group), 4 * (1 - group) + 4):
            via(r, world(1 - h, 2 * m + h, MATE_PORT[k % 4]), other + 2 * m, 2)
    return writes


def calls_of(core, writes):
    calls = []
    for n in sorted({w[3] for w in writes}):
        off = [w for w in writes if w[3] == n and w[0] // 8 != core // 8]
        on = [w for w in writes if w[3] == n and w[0] // 8 == core // 8]
        while off or on:
            take_off, off = off[:8], off[8:]
            e_off = 8
            while take_off and e_off * len(take_off) > 8:
                e_off //= 2
            first_on = e_off * len(take_off)
            take_on, on = on[:16 - first_on], on[16 - first_on:]
            e_on = 16
            while take_on and e_on * len(take_on) > 16 - first_on:
                e_on //= 2
            call, bit = [], 0
            for group, e in ((take_off, e_off), (take_on, e_on)):
                for w in group:
                    call.append(w + (((1 << e) - 1) << bit, e))
                    bit += e
            calls.append(call)
    return calls


def rank_program(g, core, T, topo):
    writes = plan()
    all_calls = {c: calls_of(c, w) for c, w in writes.items()}
    if core not in all_calls:
        return
    arriving = sum(t[5] for calls in all_calls.values() for call in calls for t in call if t[0] == core)
    rank = T.rank_of(core)

    if rank is not None:
        g.dma_start(T.src[:], T.x[:]).then_inc(T.sem.loaded, 16)
        g.dma_start(T.land[:, rank * B:(rank + 1) * B], T.x[:, rank * B:(rank + 1) * B]).then_inc(T.sem.own, 16)
        g.wait_ge(T.sem.loaded, 16)
        source = T.src
    else:
        g.wait_ge(T.sem.arrived, arriving)
        source = T.land

    leaving = 0
    for call in all_calls[core]:
        transfers = []
        for dst, src_col, dst_col, n, mask, engines in call:
            rid, pid = topo.addr(dst, core)
            transfers.append(RemoteDMATransfer(
                dst_ids=[DstId(rid=rid, pnc=pid)], dma_engine_mask=mask, remote_sem=T.sem.arrived,
                src=source[:, src_col:src_col + n * B], dst=T.land[:, dst_col:dst_col + n * B]))
            leaving += engines
        g.remote_dma_fused(transfers, local_sem=T.sem.sent)

    if rank is not None:
        g.wait_ge(T.sem.arrived, arriving)
        g.wait_ge(T.sem.own, 16)
        g.dma_start(T.y[:], T.land[:]).then_inc(T.sem.stored, 16)
        g.wait_ge(T.sem.stored, 16)
    g.wait_ge(T.sem.sent, leaving)
